import numpy as np, ml_dtypes
CORES = [37,45,53,61,69,109,117,125]
N = 8
import mx_ref
NC = 256
A = np.float32(0.03)
BF = ml_dtypes.bfloat16
def setup_inputs(rng):
    def f(*shape):
        return mx_ref.flush((rng.standard_normal(shape, dtype=np.float32) * np.exp2(rng.integers(-2, 3, shape[:-1] + (1,)))).astype(BF))
    tg = np.stack([rng.integers(0, N, (N, 128)), rng.integers(0, NC, (N, 128))], axis=2).astype(BF)
    return {"tg": tg, "x": f(N, 128, 512), "w": f(N, 128, 4 * NC)}
def setup_inputs_blocks(rng):
    d = setup_inputs(rng)
    for k in ("x", "w"): d[k] = mx_ref.spread(d[k], rng, 2)
    return d
def setup_inputs_sharp(rng):
    d = setup_inputs(rng); d["w"] = (d["w"].astype(np.float32) * 32).astype(BF)
    return d
def setup_inputs_apart(rng):
    d = setup_inputs(rng); d["w"] = mx_ref.flush((d["w"].astype(np.float32) * np.exp2(rng.permutation(np.linspace(-3, 3, N))).astype(np.float32).reshape(N, 1, 1)).astype(BF))
    return d
def reference(tg, x, w):
    W = [mx_ref.quantize(w[r]) for r in range(N)]
    y = np.zeros((N, 128, 2), np.float32)
    for j in range(N):
        X = mx_ref.quantize(x[j])
        L = [(mx_ref.matmul(X, W[r]) * A).astype(np.float64) for r in range(N)]
        m = np.max([l.max(axis=1, keepdims=True) for l in L], axis=0); s = sum(np.exp(l - m).sum(axis=1, keepdims=True) for l in L)
        t = np.array([[L[int(a) % N][i, int(c) % NC]] for i, (a, c) in enumerate(tg[j].astype(np.float32))])
        y[j] = np.concatenate([np.log(s) + m - t, np.log(s) + m], axis=1).astype(np.float32)
    return {"y": y}

@@ -1,0 +1,343 @@
+import math
+from concourse.bass import DstId, RemoteDMATransfer
+from concourse.mybir import dt, AluOpType, AxisListType, ActivationFunctionType
+
+ALL_CORES = 128
+NC = 256
+NX = 128
+LOGIT = 0.03
+G = 10.0
+MAGIC = 12582912.0
+FAR = 1e29
+SLOT = 16
+SEL = 272
+
+STEPS = """
+top00 exp00 mask0 pick00 sum00 mask1 top10 exp10 mask2 pick10 sum10 top20 exp20 mask3 pick20 sum20 top30 exp30
+top11 exp11 pick30 sum30 top21 exp21 pick11 sum11 top31 exp31 pick21 sum21 top01 exp01 ln pick31 add31 pick01 add01
+"""
+
+SCRATCH = {
+    "xt": ("sbuf", [128, 512], "bfloat16"),
+    "wt": ("sbuf", [128, 1024], "bfloat16"),
+    "xq": ("sbuf", [128, 4 * NX], "float8_e4m3fn_x4"),
+    "xp": ("sbuf", [128, 4 * NX], "uint8"),
+    "wq": ("sbuf", [128, 2 * NC], "float8_e4m3fn_x4"),
+    "wp": ("sbuf", [128, 2 * NC], "uint8"),
+    "hc": ("sbuf", [128, NC], "float8_e4m3fn_x4"),
+    "hp": ("sbuf", [128, NC], "uint8"),
+    "tgd": ("dram", [128, 2], "bfloat16"),
+    "tgh": ("dram", [128, 2], "bfloat16"),
+    "tgs": ("sbuf", [128, 8], "bfloat16"),
+    "ramp": ("sbuf", [128, NC], "bfloat16"),
+    "mask": ("sbuf", [128, 8 * NC], "bfloat16"),
+    "tv": ("sbuf", [128, 4], "float32"),
+    "pm": ("sbuf", [128, 8], "float32"),
+    "es": ("sbuf", [128, 8], "float32"),
+    "ej": ("sbuf", [128, 8 * NC], "float32"),
+    "sel": ("sbuf", [128, 8 * SEL], "float32"),
+    "cj": ("sbuf", [128, 8 * SEL], "float32"),
+    "cs": ("sbuf", [128, 4], "float32"),
+    "ca": ("sbuf", [128, 8], "float32"),
+    "cb": ("sbuf", [128, 8], "float32"),
+    "cl": ("sbuf", [128, 4], "float32"),
+    "msg": ("sbuf", [128, 4 * SLOT], "float32"),
+    "land": ("sbuf", [128, 4 * SLOT], "float32"),
+    "fm": ("sbuf", [128, 2 * SLOT - 2], "float32"),
+    "fp": ("sbuf", [128, 2 * SLOT - 2], "float32"),
+    "ft": ("sbuf", [128, 4], "float32"),
+    "fv": ("sbuf", [128, 8], "float32"),
+    "yo": ("sbuf", [128, 2], "float32"),
+    "ps": ("psum", [128, 8 * 512], "float32"),
+}
+SEMAPHORES = ["tgd", "tgl", "wl", "xl", "ramp", "v", "s", "p", "xa0", "xa1", "xa2", "xa3", "wm", "ta0", "ta1", "ta2", "ta3",
+              "st", "ls", "yd", "ht", "hs", "hw", "hl"]
+
+
+def _plan(cores, topo):
+    n = len(cores)
+    chip = [topo.chip(c) for c in cores]
+    group = [[q for q in range(n) if q == r or topo.same_plane(chip[r], chip[q])] for r in range(n)]
+    partner = {}
+    for r in range(n):
+        for q in range(n):
+            if topo.mates(chip[r], chip[q]):
+                partner[r] = q
+    for r in range(n):
+        if r not in partner:
+            q = [q for q in range(n) if q not in partner and q not in group[r]][0]
+            partner[r] = q
+            partner[q] = r
+    helpers = []
+    for r in range(n):
+        dst = cores[partner[r]]
+        cand = [k for k in range(ALL_CORES) if topo.chip(k) == chip[r] and k not in cores and topo.may_write(k, dst)]
+        near = [k for k in cand if topo.die(k) == topo.die(cores[r])]
+        far = [k for k in cand if topo.die(k) != topo.die(cores[r])]
+        helpers.append((near[0], far[0]))
+    return group, partner, helpers
+
+
+def _turn(grp, r):
+    i = grp.index(r)
+    return [grp[(i + d) % len(grp)] for d in range(1, len(grp))]
+
+
+def _dst(topo, core):
+    rid, pid, _ = topo.addr(core)
+    return DstId(rid=rid, pnc=pid)
+
+
+def _engines(mask):
+    return bin(mask).count("1")
+
+
+def _halves(mask):
+    low = 0
+    while 2 * _engines(low) < _engines(mask):
+        rest = mask & ~low
+        low |= rest & -rest
+    return low, mask & ~low
+
+
+def _codes(buf, a, b):
+    return buf[:, a:b].bitcast(dt.uint8)
+
+
+def _plane(buf, a, b):
+    return buf[:, a:b]
+
+
+def _helper(g, core, T, topo, group, partner, helpers):
+    cores = T.cores
+    for r in range(len(cores)):
+        if core not in helpers[r]:
+            continue
+        i = helpers[r].index(core)
+        peer = cores[_turn(group[r], r)[1 + i]]
+        slot = group[r].index(r)
+        rid, pid, _ = topo.addr(peer)
+        m = topo.mask(core, peer)
+        k = _engines(_halves(topo.mask(core, cores[r]) & ~m)[i])
+        g.wait_ge(T.sem.ht, 1)
+        g.remote_dma(T.tgs[:, 2 * slot:2 * slot + 2], T.tgh[:], T.sem["ta%d" % slot], T.sem.hl, pid, rid, m)
+        sent = _engines(m)
+        to = cores[partner[r]]
+        rid, pid, _ = topo.addr(to)
+        m = topo.mask(core, to)
+        a, b = NX * i, NX * (i + 1)
+        g.wait_ge(T.sem.hw, k)
+        g.remote_dma(_codes(T.wq, NC + a, NC + b), _codes(T.hc, a, b), T.sem.wm, T.sem.hl, pid, rid, m)
+        g.wait_ge(T.sem.hs, k)
+        g.remote_dma(_plane(T.wp, NC + a, NC + b), _plane(T.hp, a, b), T.sem.wm, T.sem.hl, pid, rid, m)
+        sent += 2 * _engines(m)
+        g.wait_ge(T.sem.hl, sent)
+
+
+def _queue(q, T, name):
+    seen = {}
+    count = [0]
+
+    def wait(*tokens):
+        for s, n in tokens:
+            if seen.get(s, 0) < n:
+                q.wait_ge(T.sem[s], n)
+                seen[s] = n
+
+    def done(inst):
+        count[0] += 1
+        inst.then_inc(T.sem[name], 1)
+        return (name, count[0])
+
+    return wait, done
+
+
+def rank_program(g, core, T, topo):
+    group, partner, helpers = _plan(T.cores, topo)
+    me = T.rank_of(core)
+    if me is None:
+        _helper(g, core, T, topo, group, partner, helpers)
+        return
+    ALU = AluOpType
+    ACT = ActivationFunctionType
+    X = AxisListType.X
+    cores = T.cores
+    grp = group[me]
+    mate = partner[me]
+    s0 = grp.index(me)
+    peers = _turn(grp, me)
+    slots = [grp.index(q) for q in peers[::-1]]
+    order = [s0] + slots
+    helper = helpers[me]
+    off = topo.mask(core, cores[peers[0]])
+    on = topo.mask(core, helper[0]) & ~off
+    n_off, n_on = _engines(off), _engines(on)
+    vw, vd = _queue(g.vector, T, "v")
+    sw, sd = _queue(g.scalar, T, "s")
+    pw, pd = _queue(g.tensor, T, "p")
+    gw, _g = _queue(g, T, "v")
+    yw, _y = _queue(g.sync, T, "v")
+
+    g.sync.dma_start(T.tgd[:], T.tg[:]).then_inc(T.sem.tgd, 16)
+    g.scalar.dma_start(T.xt[:], T.x[:]).then_inc(T.sem.xl, 16)
+    g.scalar.dma_start(T.wt[:], T.w[:]).then_inc(T.sem.wl, 16)
+    g.sync.dma_start(T.tgs[:, 2 * s0:2 * s0 + 2], T.tg[:]).then_inc(T.sem.tgl, 16)
+    g.iota(T.ramp[:], [[1, NC]], 0, 0, allow_small_or_imprecise_dtypes=True).then_inc(T.sem.ramp, 1)
+
+    vd(g.vector.memset(T.land[:], FAR))
+    for buf, vals in ((T.ca, (-LOGIT / G, 1.0, G, 1.0)), (T.cb, (MAGIC, -MAGIC, 0.0, -G))):
+        for i in range(4):
+            vd(g.vector.memset(buf[:, i:(i + 1 if i < 3 else 5)], vals[i]))
+    xa, xb = NX * s0, NX * (s0 + 1)
+    vw(("xl", 16))
+    vd(g.vector.quantize_mx(T.xq[:, xa:xb], T.xp[:, xa:xb], T.xt[:]))
+    vw(("wl", 16))
+    t_q = vd(g.vector.quantize_mx(T.wq[:, 0:NC], T.wp[:, 0:NC], T.wt[:]))
+    for i in range(3):
+        vd(g.vector.memset(T.cs[:, i:i + 1], math.exp(-G * i) / 32.0))
+    t_cl = vd(g.vector.memset(T.cl[:, 0:1], 32.0))
+
+    gw(("tgd", 16))
+    g.remote_dma_fused([RemoteDMATransfer(
+        dst_ids=[_dst(topo, h) for h in helper], dma_engine_mask=on & -on, remote_sem=T.sem.ht,
+        srcs=[T.tgd[:]], dsts=[T.tgh[:] for h in helper])], local_sem=T.sem.ls)
+    rid, pid, _ = topo.addr(cores[peers[0]])
+    g.remote_dma(T.tgs[:, 2 * s0:2 * s0 + 2], T.tgd[:], T.sem["ta%d" % s0], T.sem.ls, pid, rid, off)
+    sent = 1 + n_off
+    gw(t_q)
+    for q in peers:
+        for view, xbuf, wbuf, hbuf, sem in ((_codes, T.xq, T.wq, T.hc, T.sem.hw), (_plane, T.xp, T.wp, T.hp, T.sem.hs)):
+            x = view(xbuf, xa, xb)
+            parts = [RemoteDMATransfer(dst_ids=[_dst(topo, cores[q])], dma_engine_mask=off,
+                                       remote_sem=T.sem["xa%d" % s0], srcs=[x], dsts=[x])]
+            sent += n_off
+            if q == peers[0]:
+                for i in range(2):
+                    parts.append(RemoteDMATransfer(
+                        dst_ids=[_dst(topo, helper[i])], dma_engine_mask=_halves(on)[i], remote_sem=sem,
+                        srcs=[view(wbuf, NX * i, NX * (i + 1))], dsts=[view(hbuf, NX * i, NX * (i + 1))]))
+                sent += n_on
+            g.remote_dma_fused(parts, local_sem=T.sem.ls)
+
+    mm = {}
+    pw(t_q)
+    for step in STEPS.split():
+        if step.startswith("top"):
+            i, h = int(step[-2]), int(step[-1])
+            s = order[i]
+            if i:
+                pw(("xa%d" % s, 2 * n_off))
+            if h:
+                pw(("wm", 4 * n_off))
+            b = 4 * h + s
+            c = slice(NX * s, NX * (s + 1))
+            w = slice(NC * h, NC * (h + 1))
+            mm[b] = pd(g.tensor.matmul_mx(T.ps[:, 512 * b:512 * b + NC], T.xq[:, c], T.xp[:, c], T.wq[:, w], T.wp[:, w],
+                                          True, True))
+
+    tf, te, ts, tm, tc, t_mask, t_ln32 = {}, {}, {}, {}, {}, {}, []
+
+    def col(t, b):
+        return t[:, b:b + 1]
+
+    def bank(b):
+        return T.ps[:, 512 * b:512 * b + NC]
+
+    def turn(a, b):
+        return (a - b) % len(grp)
+
+    def out(b, c, step=1, n=1):
+        s, h = b % 4, b // 4
+        buf = T.land if s == s0 else T.msg
+        c += SLOT * turn(s, s0) + (6 * (1 - h) if c != 3 else 0)
+        return buf[:, c:c + (n - 1) * step + 1:step] if n > 1 else buf[:, c:c + 1]
+
+    def top(b):
+        vw(mm[b])
+        t = vd(g.vector.tensor_reduce(col(T.pm, b), bank(b), X, ALU.max))
+        vw(t)
+        tf[b] = vd(g.vector.tensor_tensor_scan(out(b, 0, 2, 5), T.ca[:, 0:5], T.cb[:, 0:5], col(T.pm, b),
+                                               ALU.mult, ALU.add))
+
+    def exps(b):
+        sw(tf[b])
+        te[b] = sd(g.scalar.activation(T.ej[:, NC * b:NC * (b + 1)], bank(b), ACT.Exp, bias=out(b, 4), scale=LOGIT,
+                                       accum_out=col(T.es, b)))
+        sw(te[b], t_cl)
+        ts[b] = sd(g.scalar.activation(out(b, 5, 2, 3), T.cs[:, 0:3], ACT.Copy, scale=col(T.es, b)))
+
+    def masks(s):
+        vw(("ramp", 1), ("tgl", 16))
+        if s != s0:
+            vw(("ta%d" % s, n_off))
+        t = vd(g.vector.tensor_scalar(col(T.tv, s), T.tgs[:, 2 * s:2 * s + 1], float(NC), T.tgs[:, 2 * s + 1:2 * s + 2],
+                                      ALU.mult, ALU.add))
+        vw(t)
+        for h, r in ((0, me), (1, mate)):
+            b = 4 * h + s
+            t_mask[b] = vd(g.vector.tensor_scalar(T.mask[:, NC * b:NC * (b + 1)], T.ramp[:], float(NC * r), col(T.tv, s),
+                                                  ALU.add, ALU.is_equal))
+
+    def pick(b):
+        vw(te[b], t_mask[b])
+        tm[b] = vd(g.vector.tensor_tensor(T.sel[:, SEL * b:SEL * b + NC], bank(b), T.mask[:, NC * b:NC * (b + 1)], ALU.mult))
+
+    def total(b):
+        h = b // 4
+        sw(tm[b])
+        if h:
+            sw(tc[b - 4])
+        acc = out(b, 3) if h else col(T.sel, SEL * (b + 4) + NC)
+        tc[b] = sd(g.scalar.activation(T.cj[:, SEL * b:SEL * b + NC + h], T.sel[:, SEL * b:SEL * b + NC + h], ACT.Copy,
+                                       accum_out=acc))
+
+    def add(b):
+        vw(tm[b], tc[b - 4])
+        tc[b] = vd(g.vector.tensor_reduce(out(b, 3), T.sel[:, SEL * b:SEL * b + NC + 1], X, ALU.add))
+
+    for step in STEPS.split():
+        if step == "ln":
+            sw(t_cl)
+            t_ln32.append(sd(g.scalar.activation(T.cl[:, 1:2], T.cl[:, 0:1], ACT.Ln)))
+        elif step.startswith("mask"):
+            masks(order[int(step[4:])])
+        else:
+            b = order[int(step[-2])] + 4 * int(step[-1])
+            {"top": top, "exp": exps, "pick": pick, "sum": total, "add": add}[step[:-2]](b)
+
+    for s in slots:
+        gw(ts[4 + s], tc[4 + s])
+        rid, pid, _ = topo.addr(cores[grp[s]])
+        a, b = SLOT * turn(s0, s), SLOT * turn(s, s0)
+        g.remote_dma(T.land[:, a + 3:a + SLOT], T.msg[:, b + 3:b + SLOT], T.sem.st, T.sem.ls, pid, rid, off)
+        sent += n_off
+    g.wait_ge(T.sem.ls, sent)
+
+    own = (ts[4 + s0], tc[4 + s0])
+    st = ("st", 3 * n_off)
+    ref, val = T.land[:, 4:4 * SLOT:2], T.land[:, 5:4 * SLOT:2]
+    vw(t_ln32[0])
+    t_c = vd(g.vector.tensor_scalar(T.fv[:, 0:1], T.cl[:, 1:2], -2.0 * G, None, ALU.add))
+    sw(*own)
+    sw(st)
+    t_nt = sd(g.scalar.activation(T.ft[:], T.land[:, 3:4 * SLOT:SLOT], ACT.Copy, scale=-LOGIT, accum_out=T.fv[:, 1:2]))
+    vw(*own)
+    vw(st)
+    t = vd(g.vector.tensor_reduce(T.fv[:, 2:3], ref, X, ALU.min))
+    vw(t)
+    t = vd(g.vector.tensor_scalar(T.fm[:], ref, -2.0 * G, T.fv[:, 2:3], ALU.add, ALU.is_equal))
+    vw(t)
+    t = vd(g.vector.tensor_tensor(T.fp[:], val, T.fm[:], ALU.mult))
+    vw(t)
+    t_sum = vd(g.vector.tensor_reduce(T.fv[:, 3:4], T.fp[:], X, ALU.add))
+    sw(t_sum)
+    t_ln = sd(g.scalar.activation(T.fv[:, 4:5], T.fv[:, 3:4], ACT.Ln))
+    vw(t_c)
+    t = vd(g.vector.tensor_scalar(T.fv[:, 6:7], T.fv[:, 2:3], -1.0, T.fv[:, 0:1], ALU.mult, ALU.add))
+    vw(t, t_nt)
+    t = vd(g.vector.tensor_tensor(T.fv[:, 5:6], T.fv[:, 6:7], T.fv[:, 1:2], ALU.add))
+    vw(t, t_ln)
+    t = vd(g.vector.tensor_scalar(T.yo[:], T.fv[:, 5:7], T.fv[:, 4:5], None, ALU.add))
+    yw(t)
+    g.sync.dma_start(T.y[:], T.yo[:]).then_inc(T.sem.yd, 16)
+    g.sync.wait_ge(T.sem.yd, 16)

@@ -9,12 +9,15 @@ LOGIT = 0.03
 G = 10.0
 MAGIC = 12582912.0
 FAR = 1e29
+BIG = 2.0 ** 40
 SLOT = 16
-SEL = 272
+BASE = NC - 4
+PART = NC + 16
 
 STEPS = """
-top00 exp00 mask0 pick00 sum00 mask1 top10 exp10 mask2 pick10 sum10 top20 exp20 mask3 pick20 sum20 top30 exp30
-top11 exp11 pick30 sum30 top21 exp21 pick11 sum11 top31 exp31 pick21 sum21 top01 exp01 ln pick31 add31 pick01 add01
+top00 ref00 exp00 abs0 abs1 mask00 pick00 mask10 top10 ref10 exp10 abs2 pick10 top20 ref20 exp20 abs3 mask20 pick20
+who mask11 mask21 cpy0 cpy1 top30 ref30 exp30 cpy2 mask30 mask31
+top11 pick30 ref11 exp11 top21 top31 ref21 exp21 cpy3 pick11 ref31 exp31 top01 pick21 ref01 exp01 ln pick31 mask01 pick01
 """
 
 SCRATCH = {
@@ -29,20 +32,23 @@ SCRATCH = {
     "tgd": ("dram", [128, 2], "bfloat16"),
     "tgh": ("dram", [128, 2], "bfloat16"),
     "tgs": ("sbuf", [128, 8], "bfloat16"),
-    "ramp": ("sbuf", [128, NC], "bfloat16"),
+    "ramp": ("sbuf", [128, NC], "float32"),
+    "away": ("sbuf", [128, 4 * NC], "bfloat16"),
     "mask": ("sbuf", [128, 8 * NC], "bfloat16"),
+    "nb": ("sbuf", [128, 4], "float32"),
+    "own": ("sbuf", [128, 4], "float32"),
+    "cut": ("sbuf", [128, 4], "float32"),
     "tv": ("sbuf", [128, 4], "float32"),
     "pm": ("sbuf", [128, 8], "float32"),
     "es": ("sbuf", [128, 8], "float32"),
     "ej": ("sbuf", [128, 8 * NC], "float32"),
-    "sel": ("sbuf", [128, 8 * SEL], "float32"),
-    "cj": ("sbuf", [128, 8 * SEL], "float32"),
+    "pj": ("sbuf", [128, 4 * NC], "float32"),
     "cs": ("sbuf", [128, 4], "float32"),
     "ca": ("sbuf", [128, 8], "float32"),
     "cb": ("sbuf", [128, 8], "float32"),
     "cl": ("sbuf", [128, 4], "float32"),
-    "msg": ("sbuf", [128, 4 * SLOT], "float32"),
-    "land": ("sbuf", [128, 4 * SLOT], "float32"),
+    "msg": ("sbuf", [128, 4 * PART], "float32"),
+    "land": ("sbuf", [128, BASE + 4 * SLOT], "float32"),
     "fm": ("sbuf", [128, 2 * SLOT - 2], "float32"),
     "fp": ("sbuf", [128, 2 * SLOT - 2], "float32"),
     "ft": ("sbuf", [128, 4], "float32"),
@@ -163,7 +169,6 @@ def rank_program(g, core, T, topo):
     X = AxisListType.X
     cores = T.cores
     grp = group[me]
-    mate = partner[me]
     s0 = grp.index(me)
     peers = _turn(grp, me)
     slots = [grp.index(q) for q in peers[::-1]]
@@ -178,13 +183,17 @@ def rank_program(g, core, T, topo):
     gw, _g = _queue(g, T, "v")
     yw, _y = _queue(g.sync, T, "v")
 
+    def turn(a, b):
+        return (a - b) % len(grp)
+
     g.sync.dma_start(T.tgd[:], T.tg[:]).then_inc(T.sem.tgd, 16)
     g.scalar.dma_start(T.xt[:], T.x[:]).then_inc(T.sem.xl, 16)
     g.scalar.dma_start(T.wt[:], T.w[:]).then_inc(T.sem.wl, 16)
     g.sync.dma_start(T.tgs[:, 2 * s0:2 * s0 + 2], T.tg[:]).then_inc(T.sem.tgl, 16)
     g.iota(T.ramp[:], [[1, NC]], 0, 0, allow_small_or_imprecise_dtypes=True).then_inc(T.sem.ramp, 1)
 
-    vd(g.vector.memset(T.land[:], FAR))
+    t_const = [vd(g.vector.memset(T.cl[:, 0:1], 32.0)), vd(g.vector.memset(T.cl[:, 2:3], -math.log(32.0)))]
+    vd(g.vector.memset(T.land[:, BASE:BASE + 4 * SLOT], FAR))
     for buf, vals in ((T.ca, (-LOGIT / G, 1.0, G, 1.0)), (T.cb, (MAGIC, -MAGIC, 0.0, -G))):
         for i in range(4):
             vd(g.vector.memset(buf[:, i:(i + 1 if i < 3 else 5)], vals[i]))
@@ -193,9 +202,9 @@ def rank_program(g, core, T, topo):
     vd(g.vector.quantize_mx(T.xq[:, xa:xb], T.xp[:, xa:xb], T.xt[:]))
     vw(("wl", 16))
     t_q = vd(g.vector.quantize_mx(T.wq[:, 0:NC], T.wp[:, 0:NC], T.wt[:]))
-    for i in range(3):
-        vd(g.vector.memset(T.cs[:, i:i + 1], math.exp(-G * i) / 32.0))
-    t_cl = vd(g.vector.memset(T.cl[:, 0:1], 32.0))
+
+    sw(("ramp", 1), t_const[1])
+    t_cs = sd(g.scalar.activation(T.cs[:, 0:3], T.ramp[:, 0:3], ACT.Exp, bias=T.cl[:, 2:3], scale=-G))
 
     gw(("tgd", 16))
     g.remote_dma_fused([RemoteDMATransfer(
@@ -235,7 +244,7 @@ def rank_program(g, core, T, topo):
             mm[b] = pd(g.tensor.matmul_mx(T.ps[:, 512 * b:512 * b + NC], T.xq[:, c], T.xp[:, c], T.wq[:, w], T.wp[:, w],
                                           True, True))
 
-    tf, te, ts, tm, tc, t_mask, t_ln32 = {}, {}, {}, {}, {}, {}, []
+    tm, tf, te, ts, tp, tc, t_away, t_mask, t_ln32, t_who = {}, {}, {}, {}, {}, {}, {}, {}, [], []
 
     def col(t, b):
         return t[:, b:b + 1]
@@ -243,97 +252,105 @@ def rank_program(g, core, T, topo):
     def bank(b):
         return T.ps[:, 512 * b:512 * b + NC]
 
-    def turn(a, b):
-        return (a - b) % len(grp)
-
-    def out(b, c, step=1, n=1):
+    def pair(b, c, n=1):
         s, h = b % 4, b // 4
         buf = T.land if s == s0 else T.msg
-        c += SLOT * turn(s, s0) + (6 * (1 - h) if c != 3 else 0)
-        return buf[:, c:c + (n - 1) * step + 1:step] if n > 1 else buf[:, c:c + 1]
+        c += BASE + PART * turn(s, s0) + 6 * (1 - h)
+        return buf[:, c:c + 2 * n - 1:2] if n > 1 else buf[:, c:c + 1]
 
     def top(b):
         vw(mm[b])
-        t = vd(g.vector.tensor_reduce(col(T.pm, b), bank(b), X, ALU.max))
-        vw(t)
-        tf[b] = vd(g.vector.tensor_tensor_scan(out(b, 0, 2, 5), T.ca[:, 0:5], T.cb[:, 0:5], col(T.pm, b),
-                                               ALU.mult, ALU.add))
+        tm[b] = vd(g.vector.tensor_reduce(col(T.pm, b), bank(b), X, ALU.max))
+
+    def ref(b):
+        vw(tm[b])
+        tf[b] = vd(g.vector.tensor_tensor_scan(pair(b, 0, 5), T.ca[:, 0:5], T.cb[:, 0:5], col(T.pm, b), ALU.mult, ALU.add))
 
     def exps(b):
         sw(tf[b])
-        te[b] = sd(g.scalar.activation(T.ej[:, NC * b:NC * (b + 1)], bank(b), ACT.Exp, bias=out(b, 4), scale=LOGIT,
+        te[b] = sd(g.scalar.activation(T.ej[:, NC * b:NC * (b + 1)], bank(b), ACT.Exp, bias=pair(b, 4), scale=LOGIT,
                                        accum_out=col(T.es, b)))
-        sw(te[b], t_cl)
-        ts[b] = sd(g.scalar.activation(out(b, 5, 2, 3), T.cs[:, 0:3], ACT.Copy, scale=col(T.es, b)))
+        sw(te[b], t_cs)
+        ts[b] = sd(g.scalar.activation(pair(b, 5, 3), T.cs[:, 0:3], ACT.Copy, scale=col(T.es, b)))
 
-    def masks(s):
-        vw(("ramp", 1), ("tgl", 16))
-        if s != s0:
-            vw(("ta%d" % s, n_off))
-        t = vd(g.vector.tensor_scalar(col(T.tv, s), T.tgs[:, 2 * s:2 * s + 1], float(NC), T.tgs[:, 2 * s + 1:2 * s + 2],
-                                      ALU.mult, ALU.add))
-        vw(t)
-        for h, r in ((0, me), (1, mate)):
-            b = 4 * h + s
-            t_mask[b] = vd(g.vector.tensor_scalar(T.mask[:, NC * b:NC * (b + 1)], T.ramp[:], float(NC * r), col(T.tv, s),
-                                                  ALU.add, ALU.is_equal))
+    def arrived(s):
+        return ("tgl", 16) if s == s0 else ("ta%d" % s, n_off)
+
+    def away(s):
+        sw(arrived(s))
+        t = sd(g.scalar.activation(col(T.nb, s), col(T.tgs, 2 * s + 1), ACT.Copy, bias=0.5 * BIG, scale=-2.0 * BIG))
+        sw(t)
+        t_away[s] = sd(g.scalar.activation(T.away[:, NC * s:NC * (s + 1)], T.ramp[:], ACT.Abs, bias=col(T.nb, s),
+                                           scale=2.0 * BIG))
+
+    def who():
+        vw(*[arrived(s) for s in order])
+        ranks = T.tgs[:, 0:8:2]
+        t_who.append(vd(g.vector.tensor_scalar(T.own[:], ranks, float(me), None, ALU.is_equal)))
+        t_who.append(vd(g.vector.tensor_scalar(T.cut[:], ranks, float(partner[me]), 1.5 * BIG, ALU.is_equal, ALU.mult)))
+
+    def mask(b):
+        s, h = b % 4, b // 4
+        vw(t_away[s])
+        if h:
+            vw(t_who[1])
+        t_mask[b] = vd(g.vector.tensor_scalar(T.mask[:, NC * b:NC * (b + 1)], T.away[:, NC * s:NC * (s + 1)],
+                                              col(T.cut, s) if h else 1.5 * BIG, 1.0, ALU.subtract, ALU.min))
 
     def pick(b):
+        s, h = b % 4, b // 4
         vw(te[b], t_mask[b])
-        tm[b] = vd(g.vector.tensor_tensor(T.sel[:, SEL * b:SEL * b + NC], bank(b), T.mask[:, NC * b:NC * (b + 1)], ALU.mult))
-
-    def total(b):
-        h = b // 4
-        sw(tm[b])
+        row, start = T.pj[:, NC * s:NC * (s + 1)], 0.0
         if h:
-            sw(tc[b - 4])
-        acc = out(b, 3) if h else col(T.sel, SEL * (b + 4) + NC)
-        tc[b] = sd(g.scalar.activation(T.cj[:, SEL * b:SEL * b + NC + h], T.sel[:, SEL * b:SEL * b + NC + h], ACT.Copy,
-                                       accum_out=acc))
+            vw(tc[s])
+            c = BASE + PART * turn(s, s0) + 4
+            row, start = (T.land if s == s0 else T.msg)[:, c - NC:c], col(T.tv, s)
+        tp[b] = vd(g.vector.tensor_tensor_scan(row, bank(b), T.mask[:, NC * b:NC * (b + 1)], start, ALU.add, ALU.mult))
 
-    def add(b):
-        vw(tm[b], tc[b - 4])
-        tc[b] = vd(g.vector.tensor_reduce(out(b, 3), T.sel[:, SEL * b:SEL * b + NC + 1], X, ALU.add))
+    def keep(s):
+        sw(tp[s], t_who[0])
+        tc[s] = sd(g.scalar.activation(col(T.tv, s), col(T.pj, NC * (s + 1) - 1), ACT.Copy, scale=col(T.own, s)))
 
     for step in STEPS.split():
         if step == "ln":
-            sw(t_cl)
+            sw(t_const[0])
             t_ln32.append(sd(g.scalar.activation(T.cl[:, 1:2], T.cl[:, 0:1], ACT.Ln)))
-        elif step.startswith("mask"):
-            masks(order[int(step[4:])])
+        elif step == "who":
+            who()
+        elif step[:-1] in ("abs", "cpy"):
+            {"abs": away, "cpy": keep}[step[:-1]](order[int(step[-1])])
         else:
             b = order[int(step[-2])] + 4 * int(step[-1])
-            {"top": top, "exp": exps, "pick": pick, "sum": total, "add": add}[step[:-2]](b)
+            {"top": top, "ref": ref, "exp": exps, "mask": mask, "pick": pick}[step[:-2]](b)
 
     for s in slots:
-        gw(ts[4 + s], tc[4 + s])
+        gw(ts[4 + s], tp[4 + s])
         rid, pid, _ = topo.addr(cores[grp[s]])
-        a, b = SLOT * turn(s0, s), SLOT * turn(s, s0)
+        a, b = BASE + SLOT * turn(s0, s), BASE + PART * turn(s, s0)
         g.remote_dma(T.land[:, a + 3:a + SLOT], T.msg[:, b + 3:b + SLOT], T.sem.st, T.sem.ls, pid, rid, off)
         sent += n_off
     g.wait_ge(T.sem.ls, sent)
 
-    own = (ts[4 + s0], tc[4 + s0])
+    end = BASE + 4 * SLOT
+    refs, vals = T.land[:, BASE + 4:end:2], T.land[:, BASE + 5:end:2]
+    own = (ts[4 + s0], tp[4 + s0])
     st = ("st", 3 * n_off)
-    ref, val = T.land[:, 4:4 * SLOT:2], T.land[:, 5:4 * SLOT:2]
-    vw(t_ln32[0])
-    t_c = vd(g.vector.tensor_scalar(T.fv[:, 0:1], T.cl[:, 1:2], -2.0 * G, None, ALU.add))
     sw(*own)
     sw(st)
-    t_nt = sd(g.scalar.activation(T.ft[:], T.land[:, 3:4 * SLOT:SLOT], ACT.Copy, scale=-LOGIT, accum_out=T.fv[:, 1:2]))
+    t_nt = sd(g.scalar.activation(T.ft[:], T.land[:, BASE + 3:end:SLOT], ACT.Copy, scale=LOGIT / BIG, accum_out=T.fv[:, 1:2]))
     vw(*own)
     vw(st)
-    t = vd(g.vector.tensor_reduce(T.fv[:, 2:3], ref, X, ALU.min))
+    t = vd(g.vector.tensor_reduce(T.fv[:, 2:3], refs, X, ALU.min, negate=True))
     vw(t)
-    t = vd(g.vector.tensor_scalar(T.fm[:], ref, -2.0 * G, T.fv[:, 2:3], ALU.add, ALU.is_equal))
+    t = vd(g.vector.tensor_scalar(T.fm[:], refs, T.fv[:, 2:3], 2.0 * G, ALU.add, ALU.is_equal))
     vw(t)
-    t = vd(g.vector.tensor_tensor(T.fp[:], val, T.fm[:], ALU.mult))
+    t = vd(g.vector.tensor_tensor(T.fp[:], vals, T.fm[:], ALU.mult))
     vw(t)
     t_sum = vd(g.vector.tensor_reduce(T.fv[:, 3:4], T.fp[:], X, ALU.add))
     sw(t_sum)
     t_ln = sd(g.scalar.activation(T.fv[:, 4:5], T.fv[:, 3:4], ACT.Ln))
-    vw(t_c)
-    t = vd(g.vector.tensor_scalar(T.fv[:, 6:7], T.fv[:, 2:3], -1.0, T.fv[:, 0:1], ALU.mult, ALU.add))
+    vw(t_ln32[0])
+    t = vd(g.vector.tensor_scalar(T.fv[:, 6:7], T.fv[:, 2:3], 2.0 * G, T.cl[:, 1:2], ALU.subtract, ALU.add))
     vw(t, t_nt)
     t = vd(g.vector.tensor_tensor(T.fv[:, 5:6], T.fv[:, 6:7], T.fv[:, 1:2], ALU.add))
     vw(t, t_ln)

import math
from concourse.bass import DstId, RemoteDMATransfer
from concourse.mybir import dt, AluOpType, AxisListType, ActivationFunctionType

ALL_CORES = 128
NC = 256
NX = 128
LOGIT = 0.03
G = 10.0
MAGIC = 12582912.0
FAR = 1e29
BIG = 2.0 ** 40
SLOT = 16
BASE = NC - 4
PART = NC + 16

STEPS = """
top00 ref00 exp00 abs0 abs1 mask00 pick00 mask10 top10 ref10 exp10 abs2 pick10 top20 ref20 exp20 abs3 mask20 pick20
who mask11 mask21 cpy0 cpy1 top30 ref30 exp30 cpy2 mask30 mask31
top11 pick30 ref11 exp11 top21 top31 ref21 exp21 cpy3 pick11 ref31 exp31 top01 pick21 ref01 exp01 ln pick31 mask01 pick01
"""

SCRATCH = {
    "xt": ("sbuf", [128, 512], "bfloat16"),
    "wt": ("sbuf", [128, 1024], "bfloat16"),
    "xq": ("sbuf", [128, 4 * NX], "float8_e4m3fn_x4"),
    "xp": ("sbuf", [128, 4 * NX], "uint8"),
    "wq": ("sbuf", [128, 2 * NC], "float8_e4m3fn_x4"),
    "wp": ("sbuf", [128, 2 * NC], "uint8"),
    "hc": ("sbuf", [128, NC], "float8_e4m3fn_x4"),
    "hp": ("sbuf", [128, NC], "uint8"),
    "tgd": ("dram", [128, 2], "bfloat16"),
    "tgh": ("dram", [128, 2], "bfloat16"),
    "tgs": ("sbuf", [128, 8], "bfloat16"),
    "ramp": ("sbuf", [128, NC], "float32"),
    "away": ("sbuf", [128, 4 * NC], "bfloat16"),
    "mask": ("sbuf", [128, 8 * NC], "bfloat16"),
    "nb": ("sbuf", [128, 4], "float32"),
    "own": ("sbuf", [128, 4], "float32"),
    "cut": ("sbuf", [128, 4], "float32"),
    "tv": ("sbuf", [128, 4], "float32"),
    "pm": ("sbuf", [128, 8], "float32"),
    "es": ("sbuf", [128, 8], "float32"),
    "ej": ("sbuf", [128, 8 * NC], "float32"),
    "pj": ("sbuf", [128, 4 * NC], "float32"),
    "cs": ("sbuf", [128, 4], "float32"),
    "ca": ("sbuf", [128, 8], "float32"),
    "cb": ("sbuf", [128, 8], "float32"),
    "cl": ("sbuf", [128, 4], "float32"),
    "msg": ("sbuf", [128, 4 * PART], "float32"),
    "land": ("sbuf", [128, BASE + 4 * SLOT], "float32"),
    "fm": ("sbuf", [128, 2 * SLOT - 2], "float32"),
    "fp": ("sbuf", [128, 2 * SLOT - 2], "float32"),
    "ft": ("sbuf", [128, 4], "float32"),
    "fv": ("sbuf", [128, 8], "float32"),
    "yo": ("sbuf", [128, 2], "float32"),
    "ps": ("psum", [128, 8 * 512], "float32"),
}
SEMAPHORES = ["tgd", "tgl", "wl", "xl", "ramp", "v", "s", "p", "xa0", "xa1", "xa2", "xa3", "wm", "ta0", "ta1", "ta2", "ta3",
              "st", "ls", "yd", "ht", "hs", "hw", "hl"]


def _plan(cores, topo):
    n = len(cores)
    chip = [topo.chip(c) for c in cores]
    group = [[q for q in range(n) if q == r or topo.same_plane(chip[r], chip[q])] for r in range(n)]
    partner = {}
    for r in range(n):
        for q in range(n):
            if topo.mates(chip[r], chip[q]):
                partner[r] = q
    for r in range(n):
        if r not in partner:
            q = [q for q in range(n) if q not in partner and q not in group[r]][0]
            partner[r] = q
            partner[q] = r
    helpers = []
    for r in range(n):
        dst = cores[partner[r]]
        cand = [k for k in range(ALL_CORES) if topo.chip(k) == chip[r] and k not in cores and topo.may_write(k, dst)]
        near = [k for k in cand if topo.die(k) == topo.die(cores[r])]
        far = [k for k in cand if topo.die(k) != topo.die(cores[r])]
        helpers.append((near[0], far[0]))
    return group, partner, helpers


def _turn(grp, r):
    i = grp.index(r)
    return [grp[(i + d) % len(grp)] for d in range(1, len(grp))]


def _dst(topo, core):
    rid, pid, _ = topo.addr(core)
    return DstId(rid=rid, pnc=pid)


def _engines(mask):
    return bin(mask).count("1")


def _halves(mask):
    low = 0
    while 2 * _engines(low) < _engines(mask):
        rest = mask & ~low
        low |= rest & -rest
    return low, mask & ~low


def _codes(buf, a, b):
    return buf[:, a:b].bitcast(dt.uint8)


def _plane(buf, a, b):
    return buf[:, a:b]


def _helper(g, core, T, topo, group, partner, helpers):
    cores = T.cores
    for r in range(len(cores)):
        if core not in helpers[r]:
            continue
        i = helpers[r].index(core)
        peer = cores[_turn(group[r], r)[1 + i]]
        slot = group[r].index(r)
        rid, pid, _ = topo.addr(peer)
        m = topo.mask(core, peer)
        k = _engines(_halves(topo.mask(core, cores[r]) & ~m)[i])
        g.wait_ge(T.sem.ht, 1)
        g.remote_dma(T.tgs[:, 2 * slot:2 * slot + 2], T.tgh[:], T.sem["ta%d" % slot], T.sem.hl, pid, rid, m)
        sent = _engines(m)
        to = cores[partner[r]]
        rid, pid, _ = topo.addr(to)
        m = topo.mask(core, to)
        a, b = NX * i, NX * (i + 1)
        g.wait_ge(T.sem.hw, k)
        g.remote_dma(_codes(T.wq, NC + a, NC + b), _codes(T.hc, a, b), T.sem.wm, T.sem.hl, pid, rid, m)
        g.wait_ge(T.sem.hs, k)
        g.remote_dma(_plane(T.wp, NC + a, NC + b), _plane(T.hp, a, b), T.sem.wm, T.sem.hl, pid, rid, m)
        sent += 2 * _engines(m)
        g.wait_ge(T.sem.hl, sent)


def _queue(q, T, name):
    seen = {}
    count = [0]

    def wait(*tokens):
        for s, n in tokens:
            if seen.get(s, 0) < n:
                q.wait_ge(T.sem[s], n)
                seen[s] = n

    def done(inst):
        count[0] += 1
        inst.then_inc(T.sem[name], 1)
        return (name, count[0])

    return wait, done


def rank_program(g, core, T, topo):
    group, partner, helpers = _plan(T.cores, topo)
    me = T.rank_of(core)
    if me is None:
        _helper(g, core, T, topo, group, partner, helpers)
        return
    ALU = AluOpType
    ACT = ActivationFunctionType
    X = AxisListType.X
    cores = T.cores
    grp = group[me]
    s0 = grp.index(me)
    peers = _turn(grp, me)
    slots = [grp.index(q) for q in peers[::-1]]
    order = [s0] + slots
    helper = helpers[me]
    off = topo.mask(core, cores[peers[0]])
    on = topo.mask(core, helper[0]) & ~off
    n_off, n_on = _engines(off), _engines(on)
    vw, vd = _queue(g.vector, T, "v")
    sw, sd = _queue(g.scalar, T, "s")
    pw, pd = _queue(g.tensor, T, "p")
    gw, _g = _queue(g, T, "v")
    yw, _y = _queue(g.sync, T, "v")

    def turn(a, b):
        return (a - b) % len(grp)

    g.sync.dma_start(T.tgd[:], T.tg[:]).then_inc(T.sem.tgd, 16)
    g.scalar.dma_start(T.xt[:], T.x[:]).then_inc(T.sem.xl, 16)
    g.scalar.dma_start(T.wt[:], T.w[:]).then_inc(T.sem.wl, 16)
    g.sync.dma_start(T.tgs[:, 2 * s0:2 * s0 + 2], T.tg[:]).then_inc(T.sem.tgl, 16)
    g.iota(T.ramp[:], [[1, NC]], 0, 0, allow_small_or_imprecise_dtypes=True).then_inc(T.sem.ramp, 1)

    t_const = [vd(g.vector.memset(T.cl[:, 0:1], 32.0)), vd(g.vector.memset(T.cl[:, 2:3], -math.log(32.0)))]
    vd(g.vector.memset(T.land[:, BASE:BASE + 4 * SLOT], FAR))
    for buf, vals in ((T.ca, (-LOGIT / G, 1.0, G, 1.0)), (T.cb, (MAGIC, -MAGIC, 0.0, -G))):
        for i in range(4):
            vd(g.vector.memset(buf[:, i:(i + 1 if i < 3 else 5)], vals[i]))
    xa, xb = NX * s0, NX * (s0 + 1)
    vw(("xl", 16))
    vd(g.vector.quantize_mx(T.xq[:, xa:xb], T.xp[:, xa:xb], T.xt[:]))
    vw(("wl", 16))
    t_q = vd(g.vector.quantize_mx(T.wq[:, 0:NC], T.wp[:, 0:NC], T.wt[:]))

    sw(("ramp", 1), t_const[1])
    t_cs = sd(g.scalar.activation(T.cs[:, 0:3], T.ramp[:, 0:3], ACT.Exp, bias=T.cl[:, 2:3], scale=-G))

    gw(("tgd", 16))
    g.remote_dma_fused([RemoteDMATransfer(
        dst_ids=[_dst(topo, h) for h in helper], dma_engine_mask=on & -on, remote_sem=T.sem.ht,
        srcs=[T.tgd[:]], dsts=[T.tgh[:] for h in helper])], local_sem=T.sem.ls)
    rid, pid, _ = topo.addr(cores[peers[0]])
    g.remote_dma(T.tgs[:, 2 * s0:2 * s0 + 2], T.tgd[:], T.sem["ta%d" % s0], T.sem.ls, pid, rid, off)
    sent = 1 + n_off
    gw(t_q)
    for q in peers:
        for view, xbuf, wbuf, hbuf, sem in ((_codes, T.xq, T.wq, T.hc, T.sem.hw), (_plane, T.xp, T.wp, T.hp, T.sem.hs)):
            x = view(xbuf, xa, xb)
            parts = [RemoteDMATransfer(dst_ids=[_dst(topo, cores[q])], dma_engine_mask=off,
                                       remote_sem=T.sem["xa%d" % s0], srcs=[x], dsts=[x])]
            sent += n_off
            if q == peers[0]:
                for i in range(2):
                    parts.append(RemoteDMATransfer(
                        dst_ids=[_dst(topo, helper[i])], dma_engine_mask=_halves(on)[i], remote_sem=sem,
                        srcs=[view(wbuf, NX * i, NX * (i + 1))], dsts=[view(hbuf, NX * i, NX * (i + 1))]))
                sent += n_on
            g.remote_dma_fused(parts, local_sem=T.sem.ls)

    mm = {}
    pw(t_q)
    for step in STEPS.split():
        if step.startswith("top"):
            i, h = int(step[-2]), int(step[-1])
            s = order[i]
            if i:
                pw(("xa%d" % s, 2 * n_off))
            if h:
                pw(("wm", 4 * n_off))
            b = 4 * h + s
            c = slice(NX * s, NX * (s + 1))
            w = slice(NC * h, NC * (h + 1))
            mm[b] = pd(g.tensor.matmul_mx(T.ps[:, 512 * b:512 * b + NC], T.xq[:, c], T.xp[:, c], T.wq[:, w], T.wp[:, w],
                                          True, True))

    tm, tf, te, ts, tp, tc, t_away, t_mask, t_ln32, t_who = {}, {}, {}, {}, {}, {}, {}, {}, [], []

    def col(t, b):
        return t[:, b:b + 1]

    def bank(b):
        return T.ps[:, 512 * b:512 * b + NC]

    def pair(b, c, n=1):
        s, h = b % 4, b // 4
        buf = T.land if s == s0 else T.msg
        c += BASE + PART * turn(s, s0) + 6 * (1 - h)
        return buf[:, c:c + 2 * n - 1:2] if n > 1 else buf[:, c:c + 1]

    def top(b):
        vw(mm[b])
        tm[b] = vd(g.vector.tensor_reduce(col(T.pm, b), bank(b), X, ALU.max))

    def ref(b):
        vw(tm[b])
        tf[b] = vd(g.vector.tensor_tensor_scan(pair(b, 0, 5), T.ca[:, 0:5], T.cb[:, 0:5], col(T.pm, b), ALU.mult, ALU.add))

    def exps(b):
        sw(tf[b])
        te[b] = sd(g.scalar.activation(T.ej[:, NC * b:NC * (b + 1)], bank(b), ACT.Exp, bias=pair(b, 4), scale=LOGIT,
                                       accum_out=col(T.es, b)))
        sw(te[b], t_cs)
        ts[b] = sd(g.scalar.activation(pair(b, 5, 3), T.cs[:, 0:3], ACT.Copy, scale=col(T.es, b)))

    def arrived(s):
        return ("tgl", 16) if s == s0 else ("ta%d" % s, n_off)

    def away(s):
        sw(arrived(s))
        t = sd(g.scalar.activation(col(T.nb, s), col(T.tgs, 2 * s + 1), ACT.Copy, bias=0.5 * BIG, scale=-2.0 * BIG))
        sw(t)
        t_away[s] = sd(g.scalar.activation(T.away[:, NC * s:NC * (s + 1)], T.ramp[:], ACT.Abs, bias=col(T.nb, s),
                                           scale=2.0 * BIG))

    def who():
        vw(*[arrived(s) for s in order])
        ranks = T.tgs[:, 0:8:2]
        t_who.append(vd(g.vector.tensor_scalar(T.own[:], ranks, float(me), None, ALU.is_equal)))
        t_who.append(vd(g.vector.tensor_scalar(T.cut[:], ranks, float(partner[me]), 1.5 * BIG, ALU.is_equal, ALU.mult)))

    def mask(b):
        s, h = b % 4, b // 4
        vw(t_away[s])
        if h:
            vw(t_who[1])
        t_mask[b] = vd(g.vector.tensor_scalar(T.mask[:, NC * b:NC * (b + 1)], T.away[:, NC * s:NC * (s + 1)],
                                              col(T.cut, s) if h else 1.5 * BIG, 1.0, ALU.subtract, ALU.min))

    def pick(b):
        s, h = b % 4, b // 4
        vw(te[b], t_mask[b])
        row, start = T.pj[:, NC * s:NC * (s + 1)], 0.0
        if h:
            vw(tc[s])
            c = BASE + PART * turn(s, s0) + 4
            row, start = (T.land if s == s0 else T.msg)[:, c - NC:c], col(T.tv, s)
        tp[b] = vd(g.vector.tensor_tensor_scan(row, bank(b), T.mask[:, NC * b:NC * (b + 1)], start, ALU.add, ALU.mult))

    def keep(s):
        sw(tp[s], t_who[0])
        tc[s] = sd(g.scalar.activation(col(T.tv, s), col(T.pj, NC * (s + 1) - 1), ACT.Copy, scale=col(T.own, s)))

    for step in STEPS.split():
        if step == "ln":
            sw(t_const[0])
            t_ln32.append(sd(g.scalar.activation(T.cl[:, 1:2], T.cl[:, 0:1], ACT.Ln)))
        elif step == "who":
            who()
        elif step[:-1] in ("abs", "cpy"):
            {"abs": away, "cpy": keep}[step[:-1]](order[int(step[-1])])
        else:
            b = order[int(step[-2])] + 4 * int(step[-1])
            {"top": top, "ref": ref, "exp": exps, "mask": mask, "pick": pick}[step[:-2]](b)

    for s in slots:
        gw(ts[4 + s], tp[4 + s])
        rid, pid, _ = topo.addr(cores[grp[s]])
        a, b = BASE + SLOT * turn(s0, s), BASE + PART * turn(s, s0)
        g.remote_dma(T.land[:, a + 3:a + SLOT], T.msg[:, b + 3:b + SLOT], T.sem.st, T.sem.ls, pid, rid, off)
        sent += n_off
    g.wait_ge(T.sem.ls, sent)

    end = BASE + 4 * SLOT
    refs, vals = T.land[:, BASE + 4:end:2], T.land[:, BASE + 5:end:2]
    own = (ts[4 + s0], tp[4 + s0])
    st = ("st", 3 * n_off)
    sw(*own)
    sw(st)
    t_nt = sd(g.scalar.activation(T.ft[:], T.land[:, BASE + 3:end:SLOT], ACT.Copy, scale=LOGIT / BIG, accum_out=T.fv[:, 1:2]))
    vw(*own)
    vw(st)
    t = vd(g.vector.tensor_reduce(T.fv[:, 2:3], refs, X, ALU.min, negate=True))
    vw(t)
    t = vd(g.vector.tensor_scalar(T.fm[:], refs, T.fv[:, 2:3], 2.0 * G, ALU.add, ALU.is_equal))
    vw(t)
    t = vd(g.vector.tensor_tensor(T.fp[:], vals, T.fm[:], ALU.mult))
    vw(t)
    t_sum = vd(g.vector.tensor_reduce(T.fv[:, 3:4], T.fp[:], X, ALU.add))
    sw(t_sum)
    t_ln = sd(g.scalar.activation(T.fv[:, 4:5], T.fv[:, 3:4], ACT.Ln))
    vw(t_ln32[0])
    t = vd(g.vector.tensor_scalar(T.fv[:, 6:7], T.fv[:, 2:3], 2.0 * G, T.cl[:, 1:2], ALU.subtract, ALU.add))
    vw(t, t_nt)
    t = vd(g.vector.tensor_tensor(T.fv[:, 5:6], T.fv[:, 6:7], T.fv[:, 1:2], ALU.add))
    vw(t, t_ln)
    t = vd(g.vector.tensor_scalar(T.yo[:], T.fv[:, 5:7], T.fv[:, 4:5], None, ALU.add))
    yw(t)
    g.sync.dma_start(T.y[:], T.yo[:]).then_inc(T.sem.yd, 16)
    g.sync.wait_ge(T.sem.yd, 16)
